import numpy as np
import ml_dtypes

BF16 = ml_dtypes.bfloat16


def bf(x):
    return np.asarray(x, np.float32).astype(BF16)


def f32(x):
    return np.asarray(x, np.float32)


def f64(x):
    return np.asarray(x).astype(np.float64)


def striped(idx):
    return np.tile(idx.reshape(-1, 16).T, (8, 1))


S, K, M, N = 1024, 128, 256, 384


def setup_inputs():
    return {"table": bf(np.random.standard_normal((S, K))), "w": bf(np.random.standard_normal((K, M)) / np.sqrt(K)), "offs": striped(np.random.permutation(S)[:N])}


def reference(table, w, offs):
    idx = offs[:16].T.reshape(-1)
    x = f64(table)[idx].T
    y = f64(w).T @ x
    return y

@@ -1,0 +1,50 @@
+import concourse.masks as masks
+import concourse.mybir as mybir
+
+P = 128
+S, K, M, N = 1024, 128, 256, 384
+S_BLOCKS = S // P
+M_BLOCKS = M // P
+
+BF16, F32, U16 = mybir.dt.bfloat16, mybir.dt.float32, mybir.dt.uint16
+
+FLOPS = 2 * K * M * N
+
+
+def tile_gather_matmul_kernel(tc, table, w, offs, out):
+    nc = tc.nc
+    with (
+        tc.tile_pool(name="held", bufs=1) as held,
+        tc.psum_pool(name="psum", bufs=1) as psum,
+    ):
+        offsets = held.tile([P, N // 16], U16, name="offsets")
+        nc.sync.dma_start(offsets[:], offs)
+
+        rows = held.tile([P, S_BLOCKS, K], BF16, name="rows")
+        nc.sync.dma_start(rows[:], table.rearrange("(b p) k -> p b k", p=P))
+
+        weights = held.tile([K, M], BF16, name="weights")
+        nc.sync.dma_start(weights[:], w)
+
+        identity = held.tile([P, P], BF16, name="identity")
+        masks.make_identity(nc, identity[:])
+
+        flipped = psum.tile([K, S], BF16, name="flipped")
+        for b in range(S_BLOCKS):
+            nc.tensor.transpose(flipped[:, b * P : (b + 1) * P], rows[:, b, :], identity[:])
+        window = held.tile([K, S], BF16, name="window")
+        nc.vector.tensor_copy(window[:], flipped[:])
+
+        staged = held.tile([P, M_BLOCKS, N], F32, name="staged")
+        for a in range(M_BLOCKS):
+            product = psum.tile([P, N], F32, name=f"product{a}")
+            nc.tensor.matmul(
+                product[:],
+                weights[:, a * P : (a + 1) * P],
+                window[:].indirect(offsets[:]),
+                start=True,
+                stop=True,
+            )
+            nc.vector.tensor_copy(staged[:, a, :], product[:])
+
+        nc.sync.dma_start(out.rearrange("(a p) j -> p a j", p=P), staged[:])

@@ -3,12 +3,15 @@ import concourse.mybir as mybir
 
 P = 128
 S, K, M, N = 1024, 128, 256, 384
-S_BLOCKS = S // P
 M_BLOCKS = M // P
 
 BF16, F32, U16 = mybir.dt.bfloat16, mybir.dt.float32, mybir.dt.uint16
 
 FLOPS = 2 * K * M * N
+
+CHUNKS = 4
+CHUNK_BLOCKS = S // P // CHUNKS
+CHUNK_S = CHUNK_BLOCKS * P
 
 
 def tile_gather_matmul_kernel(tc, table, w, offs, out):
@@ -20,8 +23,14 @@ def tile_gather_matmul_kernel(tc, table, w, offs, out):
         offsets = held.tile([P, N // 16], U16, name="offsets")
         nc.sync.dma_start(offsets[:], offs)
 
-        rows = held.tile([P, S_BLOCKS, K], BF16, name="rows")
-        nc.sync.dma_start(rows[:], table.rearrange("(b p) k -> p b k", p=P))
+        chunks = []
+        for c in range(CHUNKS):
+            rows = held.tile([P, CHUNK_BLOCKS, K], BF16, name=f"rows{c}")
+            queue = nc.sync if c % 2 == 0 else nc.scalar
+            queue.dma_start(
+                rows[:], table[c * CHUNK_S : (c + 1) * CHUNK_S, :].rearrange("(b p) k -> p b k", p=P)
+            )
+            chunks.append(rows)
 
         weights = held.tile([K, M], BF16, name="weights")
         nc.sync.dma_start(weights[:], w)
@@ -29,13 +38,17 @@ def tile_gather_matmul_kernel(tc, table, w, offs, out):
         identity = held.tile([P, P], BF16, name="identity")
         masks.make_identity(nc, identity[:])
 
-        flipped = psum.tile([K, S], BF16, name="flipped")
-        for b in range(S_BLOCKS):
-            nc.tensor.transpose(flipped[:, b * P : (b + 1) * P], rows[:, b, :], identity[:])
         window = held.tile([K, S], BF16, name="window")
-        nc.vector.tensor_copy(window[:], flipped[:])
+        for c in range(CHUNKS):
+            flipped = psum.tile([K, CHUNK_S], BF16, name=f"flipped{c}")
+            for b in range(CHUNK_BLOCKS):
+                nc.tensor.transpose(flipped[:, b * P : (b + 1) * P], chunks[c][:, b, :], identity[:])
+            columns = window[:, c * CHUNK_S : (c + 1) * CHUNK_S]
+            if c % 2 == 0:
+                nc.vector.tensor_copy(columns, flipped[:])
+            else:
+                nc.scalar.copy(columns, flipped[:])
 
-        staged = held.tile([P, M_BLOCKS, N], F32, name="staged")
         for a in range(M_BLOCKS):
             product = psum.tile([P, N], F32, name=f"product{a}")
             nc.tensor.matmul(
@@ -45,6 +58,10 @@ def tile_gather_matmul_kernel(tc, table, w, offs, out):
                 start=True,
                 stop=True,
             )
-            nc.vector.tensor_copy(staged[:, a, :], product[:])
-
-        nc.sync.dma_start(out.rearrange("(a p) j -> p a j", p=P), staged[:])
+            staged = held.tile([P, N], F32, name=f"staged{a}")
+            if a % 2 == 0:
+                nc.vector.tensor_copy(staged[:], product[:])
+                nc.sync.dma_start(out[a * P : (a + 1) * P, :], staged[:])
+            else:
+                nc.scalar.copy(staged[:], product[:])
+                nc.scalar.dma_start(out[a * P : (a + 1) * P, :], staged[:])

@@ -12,6 +12,8 @@ FLOPS = 2 * K * M * N
 CHUNKS = 4
 CHUNK_BLOCKS = S // P // CHUNKS
 CHUNK_S = CHUNK_BLOCKS * P
+BANK = 512
+WARM_MATMULS = 5
 
 
 def tile_gather_matmul_kernel(tc, table, w, offs, out):
@@ -20,6 +22,12 @@ def tile_gather_matmul_kernel(tc, table, w, offs, out):
         tc.tile_pool(name="held", bufs=1) as held,
         tc.psum_pool(name="psum", bufs=1) as psum,
     ):
+        zeros = held.tile([P, BANK], BF16, name="zeros")
+        nc.vector.memset(zeros[:], 0.0)
+        idle = psum.tile([P, BANK], F32, name="idle")
+        for i in range(WARM_MATMULS):
+            nc.tensor.matmul(idle[:], zeros[:, 0:P], zeros[:], start=True, stop=True)
+
         offsets = held.tile([P, N // 16], U16, name="offsets")
         nc.sync.dma_start(offsets[:], offs)
 
@@ -45,9 +53,9 @@ def tile_gather_matmul_kernel(tc, table, w, offs, out):
                 nc.tensor.transpose(flipped[:, b * P : (b + 1) * P], chunks[c][:, b, :], identity[:])
             columns = window[:, c * CHUNK_S : (c + 1) * CHUNK_S]
             if c % 2 == 0:
-                nc.vector.tensor_copy(columns, flipped[:])
-            else:
                 nc.scalar.copy(columns, flipped[:])
+            else:
+                nc.vector.tensor_copy(columns, flipped[:])
 
         for a in range(M_BLOCKS):
             product = psum.tile([P, N], F32, name=f"product{a}")

@@ -9,11 +9,9 @@ BF16, F32, U16 = mybir.dt.bfloat16, mybir.dt.float32, mybir.dt.uint16
 
 FLOPS = 2 * K * M * N
 
-CHUNKS = 4
-CHUNK_BLOCKS = S // P // CHUNKS
-CHUNK_S = CHUNK_BLOCKS * P
-BANK = 512
-WARM_MATMULS = 5
+CHUNK_BLOCKS = (2, 2, 2, 2)
+assert sum(CHUNK_BLOCKS) * P == S
+FLIP_BANKS = 4
 
 
 def tile_gather_matmul_kernel(tc, table, w, offs, out):
@@ -21,25 +19,21 @@ def tile_gather_matmul_kernel(tc, table, w, offs, out):
     with (
         tc.tile_pool(name="held", bufs=1) as held,
         tc.psum_pool(name="psum", bufs=1) as psum,
+        tc.psum_pool(name="flips", bufs=FLIP_BANKS) as flips,
     ):
-        zeros = held.tile([P, BANK], BF16, name="zeros")
-        nc.vector.memset(zeros[:], 0.0)
-        idle = psum.tile([P, BANK], F32, name="idle")
-        for i in range(WARM_MATMULS):
-            nc.tensor.matmul(idle[:], zeros[:, 0:P], zeros[:], start=True, stop=True)
+        chunks = []
+        first_sample = 0
+        for c, blocks in enumerate(CHUNK_BLOCKS):
+            rows = held.tile([P, blocks, K], BF16, name=f"rows{c}")
+            nc.sync.dma_start(
+                rows[:],
+                table[first_sample : first_sample + blocks * P, :].rearrange("(b p) k -> p b k", p=P),
+            )
+            chunks.append(rows)
+            first_sample += blocks * P
 
         offsets = held.tile([P, N // 16], U16, name="offsets")
         nc.sync.dma_start(offsets[:], offs)
-
-        chunks = []
-        for c in range(CHUNKS):
-            rows = held.tile([P, CHUNK_BLOCKS, K], BF16, name=f"rows{c}")
-            queue = nc.sync if c % 2 == 0 else nc.scalar
-            queue.dma_start(
-                rows[:], table[c * CHUNK_S : (c + 1) * CHUNK_S, :].rearrange("(b p) k -> p b k", p=P)
-            )
-            chunks.append(rows)
-
         weights = held.tile([K, M], BF16, name="weights")
         nc.sync.dma_start(weights[:], w)
 
@@ -47,15 +41,17 @@ def tile_gather_matmul_kernel(tc, table, w, offs, out):
         masks.make_identity(nc, identity[:])
 
         window = held.tile([K, S], BF16, name="window")
-        for c in range(CHUNKS):
-            flipped = psum.tile([K, CHUNK_S], BF16, name=f"flipped{c}")
-            for b in range(CHUNK_BLOCKS):
+        first_sample = 0
+        for c, blocks in enumerate(CHUNK_BLOCKS):
+            flipped = flips.tile([K, blocks * P], BF16, name="flipped")
+            for b in range(blocks):
                 nc.tensor.transpose(flipped[:, b * P : (b + 1) * P], chunks[c][:, b, :], identity[:])
-            columns = window[:, c * CHUNK_S : (c + 1) * CHUNK_S]
-            if c % 2 == 0:
-                nc.scalar.copy(columns, flipped[:])
-            else:
+            columns = window[:, first_sample : first_sample + blocks * P]
+            if c % 2 == 1:
                 nc.vector.tensor_copy(columns, flipped[:])
+            else:
+                nc.scalar.copy(columns, flipped[:])
+            first_sample += blocks * P
 
         for a in range(M_BLOCKS):
             product = psum.tile([P, N], F32, name=f"product{a}")

@@ -12,6 +12,8 @@ FLOPS = 2 * K * M * N
 CHUNK_BLOCKS = (2, 2, 2, 2)
 assert sum(CHUNK_BLOCKS) * P == S
 FLIP_BANKS = 4
+PIECES = 2
+PIECE_N = N // PIECES
 
 
 def tile_gather_matmul_kernel(tc, table, w, offs, out):
@@ -27,7 +29,7 @@ def tile_gather_matmul_kernel(tc, table, w, offs, out):
             rows = held.tile([P, blocks, K], BF16, name=f"rows{c}")
             nc.sync.dma_start(
                 rows[:],
-                table[first_sample : first_sample + blocks * P, :].rearrange("(b p) k -> p b k", p=P),
+                table[first_sample : first_sample + blocks * P, :].rearrange("(p b) k -> p b k", p=P),
             )
             chunks.append(rows)
             first_sample += blocks * P
@@ -46,26 +48,24 @@ def tile_gather_matmul_kernel(tc, table, w, offs, out):
             flipped = flips.tile([K, blocks * P], BF16, name="flipped")
             for b in range(blocks):
                 nc.tensor.transpose(flipped[:, b * P : (b + 1) * P], chunks[c][:, b, :], identity[:])
-            columns = window[:, first_sample : first_sample + blocks * P]
+            columns = window[:, first_sample : first_sample + blocks * P].rearrange("k (p b) -> k p b", b=blocks)
+            in_order = flipped[:].rearrange("k (b p) -> k p b", b=blocks)
             if c % 2 == 1:
-                nc.vector.tensor_copy(columns, flipped[:])
+                nc.vector.tensor_copy(columns, in_order)
             else:
-                nc.scalar.copy(columns, flipped[:])
+                nc.scalar.copy(columns, in_order)
             first_sample += blocks * P
 
-        for a in range(M_BLOCKS):
-            product = psum.tile([P, N], F32, name=f"product{a}")
-            nc.tensor.matmul(
-                product[:],
-                weights[:, a * P : (a + 1) * P],
-                window[:].indirect(offsets[:]),
-                start=True,
-                stop=True,
-            )
-            staged = held.tile([P, N], F32, name=f"staged{a}")
-            if a % 2 == 0:
-                nc.vector.tensor_copy(staged[:], product[:])
-                nc.sync.dma_start(out[a * P : (a + 1) * P, :], staged[:])
-            else:
-                nc.scalar.copy(staged[:], product[:])
-                nc.scalar.dma_start(out[a * P : (a + 1) * P, :], staged[:])
+        for h in range(PIECES):
+            picked = window[:].indirect(offsets[:, h * (PIECE_N // 16) : (h + 1) * (PIECE_N // 16)])
+            for a in range(M_BLOCKS):
+                product = psum.tile([P, PIECE_N], F32, name=f"product{h}{a}")
+                nc.tensor.matmul(product[:], weights[:, a * P : (a + 1) * P], picked, start=True, stop=True)
+                staged = held.tile([P, PIECE_N], F32, name=f"staged{h}{a}")
+                leaves = out[a * P : (a + 1) * P, h * PIECE_N : (h + 1) * PIECE_N]
+                if a % 2 == 0:
+                    nc.vector.tensor_copy(staged[:], product[:])
+                    nc.sync.dma_start(leaves, staged[:])
+                else:
+                    nc.scalar.copy(staged[:], product[:])
+                    nc.scalar.dma_start(leaves, staged[:])

@@ -14,15 +14,23 @@ assert sum(CHUNK_BLOCKS) * P == S
 FLIP_BANKS = 4
 PIECES = 2
 PIECE_N = N // PIECES
+BANK_F32 = 512
+IDLE_MATMULS = 3
 
 
 def tile_gather_matmul_kernel(tc, table, w, offs, out):
     nc = tc.nc
     with (
         tc.tile_pool(name="held", bufs=1) as held,
-        tc.psum_pool(name="psum", bufs=1) as psum,
         tc.psum_pool(name="flips", bufs=FLIP_BANKS) as flips,
     ):
+        zeros = held.tile([P, BANK_F32], BF16, name="zeros")
+        nc.vector.memset(zeros[:], 0.0)
+        with tc.psum_pool(name="idle", bufs=1) as idle:
+            nothing = idle.tile([P, BANK_F32], F32, name="nothing")
+            for _ in range(IDLE_MATMULS):
+                nc.tensor.matmul(nothing[:], zeros[:, :P], zeros[:], start=True, stop=True)
+
         chunks = []
         first_sample = 0
         for c, blocks in enumerate(CHUNK_BLOCKS):
@@ -56,16 +64,17 @@ def tile_gather_matmul_kernel(tc, table, w, offs, out):
                 nc.scalar.copy(columns, in_order)
             first_sample += blocks * P
 
-        for h in range(PIECES):
-            picked = window[:].indirect(offsets[:, h * (PIECE_N // 16) : (h + 1) * (PIECE_N // 16)])
-            for a in range(M_BLOCKS):
-                product = psum.tile([P, PIECE_N], F32, name=f"product{h}{a}")
-                nc.tensor.matmul(product[:], weights[:, a * P : (a + 1) * P], picked, start=True, stop=True)
-                staged = held.tile([P, PIECE_N], F32, name=f"staged{h}{a}")
-                leaves = out[a * P : (a + 1) * P, h * PIECE_N : (h + 1) * PIECE_N]
-                if a % 2 == 0:
-                    nc.vector.tensor_copy(staged[:], product[:])
-                    nc.sync.dma_start(leaves, staged[:])
-                else:
-                    nc.scalar.copy(staged[:], product[:])
-                    nc.scalar.dma_start(leaves, staged[:])
+        with tc.psum_pool(name="psum", bufs=1) as psum:
+            for h in range(PIECES):
+                picked = window[:].indirect(offsets[:, h * (PIECE_N // 16) : (h + 1) * (PIECE_N // 16)])
+                for a in range(M_BLOCKS):
+                    product = psum.tile([P, PIECE_N], F32, name=f"product{h}{a}")
+                    nc.tensor.matmul(product[:], weights[:, a * P : (a + 1) * P], picked, start=True, stop=True)
+                    staged = held.tile([P, PIECE_N], F32, name=f"staged{h}{a}")
+                    leaves = out[a * P : (a + 1) * P, h * PIECE_N : (h + 1) * PIECE_N]
+                    if a % 2 == 0:
+                        nc.vector.tensor_copy(staged[:], product[:])
+                        nc.sync.dma_start(leaves, staged[:])
+                    else:
+                        nc.scalar.copy(staged[:], product[:])
+                        nc.scalar.dma_start(leaves, staged[:])

@@ -12,6 +12,7 @@ FLOPS = 2 * K * M * N
 CHUNK_BLOCKS = (2, 2, 2, 2)
 assert sum(CHUNK_BLOCKS) * P == S
 FLIP_BANKS = 4
+RUN = 4
 PIECES = 2
 PIECE_N = N // PIECES
 BANK_F32 = 512
@@ -56,12 +57,14 @@ def tile_gather_matmul_kernel(tc, table, w, offs, out):
             flipped = flips.tile([K, blocks * P], BF16, name="flipped")
             for b in range(blocks):
                 nc.tensor.transpose(flipped[:, b * P : (b + 1) * P], chunks[c][:, b, :], identity[:])
-            columns = window[:, first_sample : first_sample + blocks * P].rearrange("k (p b) -> k p b", b=blocks)
-            in_order = flipped[:].rearrange("k (b p) -> k p b", b=blocks)
+            columns = window[:, first_sample : first_sample + blocks * P].rearrange(
+                "k (g r b) -> k g b r", r=RUN, b=blocks
+            )
+            runs = flipped[:].rearrange("k (b g r) -> k g b r", b=blocks, r=RUN)
             if c % 2 == 1:
-                nc.vector.tensor_copy(columns, in_order)
+                nc.vector.tensor_copy(columns, runs)
             else:
-                nc.scalar.copy(columns, in_order)
+                nc.scalar.copy(columns, runs)
             first_sample += blocks * P
 
         with tc.psum_pool(name="psum", bufs=1) as psum:

@@ -27,6 +27,8 @@ def tile_gather_matmul_kernel(tc, table, w, offs, out):
     ):
         zeros = held.tile([P, BANK_F32], BF16, name="zeros")
         nc.vector.memset(zeros[:], 0.0)
+        early = held.tile([P, 1], BF16, name="early")
+        nc.scalar.copy(early[:], zeros[:, 0:1])
         with tc.psum_pool(name="idle", bufs=1) as idle:
             nothing = idle.tile([P, BANK_F32], F32, name="nothing")
             for _ in range(IDLE_MATMULS):

@@ -70,16 +70,14 @@ def tile_gather_matmul_kernel(tc, table, w, offs, out):
             first_sample += blocks * P
 
         with tc.psum_pool(name="psum", bufs=1) as psum:
-            for h in range(PIECES):
-                picked = window[:].indirect(offsets[:, h * (PIECE_N // 16) : (h + 1) * (PIECE_N // 16)])
-                for a in range(M_BLOCKS):
-                    product = psum.tile([P, PIECE_N], F32, name=f"product{h}{a}")
+            for a in range(M_BLOCKS):
+                staged = held.tile([P, N], F32, name=f"staged{a}")
+                for h in range(PIECES):
+                    picked = window[:].indirect(offsets[:, h * (PIECE_N // 16) : (h + 1) * (PIECE_N // 16)])
+                    product = psum.tile([P, PIECE_N], F32, name=f"product{a}{h}")
                     nc.tensor.matmul(product[:], weights[:, a * P : (a + 1) * P], picked, start=True, stop=True)
-                    staged = held.tile([P, PIECE_N], F32, name=f"staged{h}{a}")
-                    leaves = out[a * P : (a + 1) * P, h * PIECE_N : (h + 1) * PIECE_N]
-                    if a % 2 == 0:
-                        nc.vector.tensor_copy(staged[:], product[:])
-                        nc.sync.dma_start(leaves, staged[:])
+                    if h % 2 == 0:
+                        nc.scalar.copy(staged[:, h * PIECE_N : (h + 1) * PIECE_N], product[:])
                     else:
-                        nc.scalar.copy(staged[:], product[:])
-                        nc.scalar.dma_start(leaves, staged[:])
+                        nc.vector.tensor_copy(staged[:, h * PIECE_N : (h + 1) * PIECE_N], product[:])
+                nc.sync.dma_start(out[a * P : (a + 1) * P, :], staged[:])

@@ -11,6 +11,7 @@ FLOPS = 2 * K * M * N
 
 CHUNK_BLOCKS = (2, 2, 2, 2)
 assert sum(CHUNK_BLOCKS) * P == S
+LAST_CHUNK = len(CHUNK_BLOCKS) - 1
 FLIP_BANKS = 4
 RUN = 4
 PIECES = 2
@@ -38,10 +39,11 @@ def tile_gather_matmul_kernel(tc, table, w, offs, out):
         first_sample = 0
         for c, blocks in enumerate(CHUNK_BLOCKS):
             rows = held.tile([P, blocks, K], BF16, name=f"rows{c}")
-            nc.sync.dma_start(
-                rows[:],
-                table[first_sample : first_sample + blocks * P, :].rearrange("(p b) k -> p b k", p=P),
-            )
+            samples = table[first_sample : first_sample + blocks * P, :]
+            if c == LAST_CHUNK:
+                nc.sync.dma_start(rows[:], samples.rearrange("(b p) k -> p b k", p=P))
+            else:
+                nc.sync.dma_start(rows[:], samples.rearrange("(p b) k -> p b k", p=P))
             chunks.append(rows)
             first_sample += blocks * P
 
@@ -59,10 +61,11 @@ def tile_gather_matmul_kernel(tc, table, w, offs, out):
             flipped = flips.tile([K, blocks * P], BF16, name="flipped")
             for b in range(blocks):
                 nc.tensor.transpose(flipped[:, b * P : (b + 1) * P], chunks[c][:, b, :], identity[:])
-            columns = window[:, first_sample : first_sample + blocks * P].rearrange(
-                "k (g r b) -> k g b r", r=RUN, b=blocks
-            )
-            runs = flipped[:].rearrange("k (b g r) -> k g b r", b=blocks, r=RUN)
+            columns = window[:, first_sample : first_sample + blocks * P]
+            runs = flipped[:]
+            if c != LAST_CHUNK:
+                columns = columns.rearrange("k (g r b) -> k g b r", r=RUN, b=blocks)
+                runs = runs.rearrange("k (b g r) -> k g b r", b=blocks, r=RUN)
             if c % 2 == 1:
                 nc.vector.tensor_copy(columns, runs)
             else:

@@ -78,6 +78,8 @@ def tile_gather_matmul_kernel(tc, table, w, offs, out):
                 for h in range(PIECES):
                     picked = window[:].indirect(offsets[:, h * (PIECE_N // 16) : (h + 1) * (PIECE_N // 16)])
                     product = psum.tile([P, PIECE_N], F32, name=f"product{a}{h}")
+                    if (a, h) == (0, 0):
+                        nc.tensor.matmul(product[:, :16], weights[:, :P], window[:, 256:272], start=True, stop=True)
                     nc.tensor.matmul(product[:], weights[:, a * P : (a + 1) * P], picked, start=True, stop=True)
                     if h % 2 == 0:
                         nc.scalar.copy(staged[:, h * PIECE_N : (h + 1) * PIECE_N], product[:])

@@ -12,10 +12,10 @@ FLOPS = 2 * K * M * N
 CHUNK_BLOCKS = (2, 2, 2, 2)
 assert sum(CHUNK_BLOCKS) * P == S
 LAST_CHUNK = len(CHUNK_BLOCKS) - 1
-FLIP_BANKS = 4
+BANKS = 8
 RUN = 4
-PIECES = 2
-PIECE_N = N // PIECES
+PIECES = (256, 128)
+assert sum(PIECES) == N
 BANK_F32 = 512
 IDLE_MATMULS = 3
 
@@ -24,16 +24,18 @@ def tile_gather_matmul_kernel(tc, table, w, offs, out):
     nc = tc.nc
     with (
         tc.tile_pool(name="held", bufs=1) as held,
-        tc.psum_pool(name="flips", bufs=FLIP_BANKS) as flips,
+        tc.psum_pool(name="banks", bufs=BANKS) as banks,
     ):
-        zeros = held.tile([P, BANK_F32], BF16, name="zeros")
+        zeros = held.tile([P, P], BF16, name="zeros")
         nc.vector.memset(zeros[:], 0.0)
+        repeats = BANK_F32 // P
         early = held.tile([P, 1], BF16, name="early")
         nc.scalar.copy(early[:], zeros[:, 0:1])
-        with tc.psum_pool(name="idle", bufs=1) as idle:
-            nothing = idle.tile([P, BANK_F32], F32, name="nothing")
-            for _ in range(IDLE_MATMULS):
-                nc.tensor.matmul(nothing[:], zeros[:, :P], zeros[:], start=True, stop=True)
+        nothing = banks.tile([P, repeats, P], F32, name="nothing", tag="bank")
+        for _ in range(IDLE_MATMULS):
+            nc.tensor.matmul(
+                nothing[:], zeros[:], zeros[:].unsqueeze(1).to_broadcast([P, repeats, P]), start=True, stop=True
+            )
 
         chunks = []
         first_sample = 0
@@ -57,32 +59,39 @@ def tile_gather_matmul_kernel(tc, table, w, offs, out):
 
         window = held.tile([K, S], BF16, name="window")
         first_sample = 0
-        for c, blocks in enumerate(CHUNK_BLOCKS):
-            flipped = flips.tile([K, blocks * P], BF16, name="flipped")
+        for c in range(LAST_CHUNK):
+            blocks = CHUNK_BLOCKS[c]
+            flipped = banks.tile([K, blocks * P], BF16, name=f"flipped{c}", tag="bank")
             for b in range(blocks):
                 nc.tensor.transpose(flipped[:, b * P : (b + 1) * P], chunks[c][:, b, :], identity[:])
-            columns = window[:, first_sample : first_sample + blocks * P]
-            runs = flipped[:]
-            if c != LAST_CHUNK:
-                columns = columns.rearrange("k (g r b) -> k g b r", r=RUN, b=blocks)
-                runs = runs.rearrange("k (b g r) -> k g b r", b=blocks, r=RUN)
+            columns = window[:, first_sample : first_sample + blocks * P].rearrange(
+                "k (g r b) -> k g b r", r=RUN, b=blocks
+            )
+            runs = flipped[:].rearrange("k (b g r) -> k g b r", b=blocks, r=RUN)
             if c % 2 == 1:
                 nc.vector.tensor_copy(columns, runs)
             else:
                 nc.scalar.copy(columns, runs)
             first_sample += blocks * P
+        for b in range(CHUNK_BLOCKS[LAST_CHUNK]):
+            flipped = banks.tile([K, P], BF16, name=f"last_flipped{b}", tag="bank")
+            nc.tensor.transpose(flipped[:], chunks[LAST_CHUNK][:, b, :], identity[:])
+            nc.vector.tensor_copy(window[:, first_sample : first_sample + P], flipped[:])
+            first_sample += P
 
-        with tc.psum_pool(name="psum", bufs=1) as psum:
-            for a in range(M_BLOCKS):
-                staged = held.tile([P, N], F32, name=f"staged{a}")
-                for h in range(PIECES):
-                    picked = window[:].indirect(offsets[:, h * (PIECE_N // 16) : (h + 1) * (PIECE_N // 16)])
-                    product = psum.tile([P, PIECE_N], F32, name=f"product{a}{h}")
-                    if (a, h) == (0, 0):
-                        nc.tensor.matmul(product[:, :16], weights[:, :P], window[:, 256:272], start=True, stop=True)
-                    nc.tensor.matmul(product[:], weights[:, a * P : (a + 1) * P], picked, start=True, stop=True)
-                    if h % 2 == 0:
-                        nc.scalar.copy(staged[:, h * PIECE_N : (h + 1) * PIECE_N], product[:])
-                    else:
-                        nc.vector.tensor_copy(staged[:, h * PIECE_N : (h + 1) * PIECE_N], product[:])
-                nc.sync.dma_start(out[a * P : (a + 1) * P, :], staged[:])
+        for a in range(M_BLOCKS):
+            block_weights = weights[:, a * P : (a + 1) * P]
+            staged = held.tile([P, N], F32, name=f"staged{a}")
+            first = 0
+            for h, piece in enumerate(PIECES):
+                picked = window[:].indirect(offsets[:, first // 16 : (first + piece) // 16])
+                product = banks.tile([P, piece], F32, name=f"product{a}{h}", tag="bank")
+                if (a, h) == (0, 0):
+                    nc.tensor.matmul(product[:, :16], block_weights, window[:, 512:528], start=True, stop=True)
+                nc.tensor.matmul(product[:], block_weights, picked, start=True, stop=True)
+                if h % 2 == 0:
+                    nc.scalar.copy(staged[:, first : first + piece], product[:])
+                else:
+                    nc.vector.tensor_copy(staged[:, first : first + piece], product[:])
+                first += piece
+            nc.sync.dma_start(out[a * P : (a + 1) * P, :], staged[:])

@@ -68,7 +68,7 @@ def tile_gather_matmul_kernel(tc, table, w, offs, out):
                 "k (g r b) -> k g b r", r=RUN, b=blocks
             )
             runs = flipped[:].rearrange("k (b g r) -> k g b r", b=blocks, r=RUN)
-            if c % 2 == 1:
+            if c > 0:
                 nc.vector.tensor_copy(columns, runs)
             else:
                 nc.scalar.copy(columns, runs)
@@ -76,7 +76,10 @@ def tile_gather_matmul_kernel(tc, table, w, offs, out):
         for b in range(CHUNK_BLOCKS[LAST_CHUNK]):
             flipped = banks.tile([K, P], BF16, name=f"last_flipped{b}", tag="bank")
             nc.tensor.transpose(flipped[:], chunks[LAST_CHUNK][:, b, :], identity[:])
-            nc.vector.tensor_copy(window[:, first_sample : first_sample + P], flipped[:])
+            if b == 0:
+                nc.scalar.copy(window[:, first_sample : first_sample + P], flipped[:])
+            else:
+                nc.vector.tensor_copy(window[:, first_sample : first_sample + P], flipped[:])
             first_sample += P
 
         for a in range(M_BLOCKS):
@@ -87,7 +90,7 @@ def tile_gather_matmul_kernel(tc, table, w, offs, out):
                 picked = window[:].indirect(offsets[:, first // 16 : (first + piece) // 16])
                 product = banks.tile([P, piece], F32, name=f"product{a}{h}", tag="bank")
                 if (a, h) == (0, 0):
-                    nc.tensor.matmul(product[:, :16], block_weights, window[:, 512:528], start=True, stop=True)
+                    nc.tensor.matmul(product[:, :16], block_weights, window[:, 768:784], start=True, stop=True)
                 nc.tensor.matmul(product[:], block_weights, picked, start=True, stop=True)
                 if h % 2 == 0:
                     nc.scalar.copy(staged[:, first : first + piece], product[:])

import concourse.masks as masks
import concourse.mybir as mybir

P = 128
S, K, M, N = 1024, 128, 256, 384
M_BLOCKS = M // P

BF16, F32, U16 = mybir.dt.bfloat16, mybir.dt.float32, mybir.dt.uint16

FLOPS = 2 * K * M * N

CHUNK_BLOCKS = (2, 2, 2, 2)
assert sum(CHUNK_BLOCKS) * P == S
LAST_CHUNK = len(CHUNK_BLOCKS) - 1
BANKS = 8
RUN = 4
PIECES = (256, 128)
assert sum(PIECES) == N
BANK_F32 = 512
IDLE_MATMULS = 3


def tile_gather_matmul_kernel(tc, table, w, offs, out):
    nc = tc.nc
    with (
        tc.tile_pool(name="held", bufs=1) as held,
        tc.psum_pool(name="banks", bufs=BANKS) as banks,
    ):
        zeros = held.tile([P, P], BF16, name="zeros")
        nc.vector.memset(zeros[:], 0.0)
        repeats = BANK_F32 // P
        early = held.tile([P, 1], BF16, name="early")
        nc.scalar.copy(early[:], zeros[:, 0:1])
        nothing = banks.tile([P, repeats, P], F32, name="nothing", tag="bank")
        for _ in range(IDLE_MATMULS):
            nc.tensor.matmul(
                nothing[:], zeros[:], zeros[:].unsqueeze(1).to_broadcast([P, repeats, P]), start=True, stop=True
            )

        chunks = []
        first_sample = 0
        for c, blocks in enumerate(CHUNK_BLOCKS):
            rows = held.tile([P, blocks, K], BF16, name=f"rows{c}")
            samples = table[first_sample : first_sample + blocks * P, :]
            if c == LAST_CHUNK:
                nc.sync.dma_start(rows[:], samples.rearrange("(b p) k -> p b k", p=P))
            else:
                nc.sync.dma_start(rows[:], samples.rearrange("(p b) k -> p b k", p=P))
            chunks.append(rows)
            first_sample += blocks * P

        offsets = held.tile([P, N // 16], U16, name="offsets")
        nc.sync.dma_start(offsets[:], offs)
        weights = held.tile([K, M], BF16, name="weights")
        nc.sync.dma_start(weights[:], w)

        identity = held.tile([P, P], BF16, name="identity")
        masks.make_identity(nc, identity[:])

        window = held.tile([K, S], BF16, name="window")
        first_sample = 0
        for c in range(LAST_CHUNK):
            blocks = CHUNK_BLOCKS[c]
            flipped = banks.tile([K, blocks * P], BF16, name=f"flipped{c}", tag="bank")
            for b in range(blocks):
                nc.tensor.transpose(flipped[:, b * P : (b + 1) * P], chunks[c][:, b, :], identity[:])
            columns = window[:, first_sample : first_sample + blocks * P].rearrange(
                "k (g r b) -> k g b r", r=RUN, b=blocks
            )
            runs = flipped[:].rearrange("k (b g r) -> k g b r", b=blocks, r=RUN)
            if c > 0:
                nc.vector.tensor_copy(columns, runs)
            else:
                nc.scalar.copy(columns, runs)
            first_sample += blocks * P
        for b in range(CHUNK_BLOCKS[LAST_CHUNK]):
            flipped = banks.tile([K, P], BF16, name=f"last_flipped{b}", tag="bank")
            nc.tensor.transpose(flipped[:], chunks[LAST_CHUNK][:, b, :], identity[:])
            if b == 0:
                nc.scalar.copy(window[:, first_sample : first_sample + P], flipped[:])
            else:
                nc.vector.tensor_copy(window[:, first_sample : first_sample + P], flipped[:])
            first_sample += P

        for a in range(M_BLOCKS):
            block_weights = weights[:, a * P : (a + 1) * P]
            staged = held.tile([P, N], F32, name=f"staged{a}")
            first = 0
            for h, piece in enumerate(PIECES):
                picked = window[:].indirect(offsets[:, first // 16 : (first + piece) // 16])
                product = banks.tile([P, piece], F32, name=f"product{a}{h}", tag="bank")
                if (a, h) == (0, 0):
                    nc.tensor.matmul(product[:, :16], block_weights, window[:, 768:784], start=True, stop=True)
                nc.tensor.matmul(product[:], block_weights, picked, start=True, stop=True)
                if h % 2 == 0:
                    nc.scalar.copy(staged[:, first : first + piece], product[:])
                else:
                    nc.vector.tensor_copy(staged[:, first : first + piece], product[:])
                first += piece
            nc.sync.dma_start(out[a * P : (a + 1) * P, :], staged[:])
